import numpy as np
import ml_dtypes


def mxq(x, axis, fmt="e4m3"):
    dtype, down = {"e4m3": (ml_dtypes.float8_e4m3fn, 7), "e5m2": (ml_dtypes.float8_e5m2, 14)}[fmt]
    v = np.moveaxis(np.asarray(x, np.float32).astype(ml_dtypes.bfloat16).astype(np.float64), axis, -1)
    blocks = v.reshape(v.shape[:-1] + (-1, 32))
    amax = np.abs(blocks).max(-1, keepdims=True)
    byte = np.maximum(np.where(amax > 0, np.frexp(amax)[1] - 1 + 127, 0) - down, 1)
    scale = np.exp2(byte - 127.0)
    codes = (blocks / scale).astype(np.float32).astype(dtype).astype(np.float64)
    return np.moveaxis((codes * scale).reshape(v.shape), -1, axis)


WIDE = False


def mx_kscale(k):
    if not WIDE:
        return np.ones(k)
    levels = np.array([10, -10, 5, -5, 0])
    if k % 512:
        return np.exp2(np.random.permutation(np.resize(levels, k // 32))).repeat(32)
    a = np.empty((k // 512, 16))
    for p in range(k // 512):
        a[p, :8] = np.random.permutation(np.resize(levels, 8))
        for g in range(8):
            far = levels[np.abs(levels - a[p, g]) >= 10]
            a[p, g + 8] = far[np.random.randint(len(far))]
    return np.exp2(a.ravel()).repeat(32)


def f64(x):
    return np.asarray(x).astype(np.float64)


def striped(idx):
    return np.tile(idx.reshape(-1, 16).T, (8, 1)).astype(np.uint16)


def unstriped(offs):
    return offs[:16].T.reshape(-1).astype(np.int64)


E2M1 = np.array([0.0, 0.5, 1.0, 1.5, 2.0, 3.0, 4.0, 6.0, -0.0, -0.5, -1.0, -1.5, -2.0, -3.0, -4.0, -6.0])


def pack_weight(w, fmt):
    k, n = w.shape
    w = f64(np.asarray(w, np.float32).astype(ml_dtypes.bfloat16)).reshape(k // 32, 32, n)
    amax = np.abs(w).max(1)
    if fmt == "e4m3":
        byte = np.frexp(amax)[1] - 1 + 127 - 7
    else:
        mant, ex = np.frexp(amax / 6.0)
        byte = np.where(mant > 0.5, ex, ex - 1) + 127
    byte = np.clip(np.where(amax > 0, byte, 1), 1, 254)
    scaled = (w * np.exp2(127.0 - byte)[:, None, :]).reshape(k, n).astype(np.float32)
    by_word = np.ascontiguousarray(scaled.reshape(k // 512, 128, 4, n).transpose(0, 1, 3, 2))
    if fmt == "e4m3":
        words = by_word.astype(ml_dtypes.float8_e4m3fn).view(np.uint8)
    else:
        c = by_word.astype(ml_dtypes.float4_e2m1fn).view(np.uint8) & 0xF
        words = (c[..., 0::2] | (c[..., 1::2] << 4)).reshape(k // 512, 128, 2 * n)
    return np.ascontiguousarray(words), np.ascontiguousarray(byte.astype(np.uint8).reshape(k // 512, 16, n))


def unpack_weight(words, scales, fmt):
    g, _, n = scales.shape
    words = np.ascontiguousarray(words).reshape(g, 128, n, -1)
    if fmt == "e4m3":
        vals = words.view(ml_dtypes.float8_e4m3fn).astype(np.float64)
    else:
        nib = np.empty((g, 128, n, 4), np.uint8)
        nib[..., 0::2] = words & 0xF
        nib[..., 1::2] = words >> 4
        vals = E2M1[nib]
    vals = vals * np.repeat(np.exp2(scales.astype(np.float64) - 127.0), 8, axis=1)[..., None]
    return vals.transpose(0, 1, 3, 2).reshape(g * 512, n)


K, T, E, C, N = 1024, 512, 12, 128, 128


def by_expert(wq, xq):
    return np.concatenate([wq[e].T @ xq[:, e * C:(e + 1) * C] for e in range(E)], axis=1)


def setup_inputs():
    n = np.random.standard_normal
    s = mx_kscale(K)
    slot_token = np.concatenate([np.random.permutation(T)[:C] for e in range(E)])
    x = pack_weight(n((K, T)) * s[:, None], "e4m3")
    wq = [pack_weight(m, "e4m3") for m in n((E, K, N)) / np.sqrt(K) / s[None, :, None]]
    wv = [pack_weight(m, "e4m3") for m in n((E, K, N)) / np.sqrt(K) / s[None, :, None]]
    return {
        "x_words": x[0],
        "x_scales": x[1],
        "wq_words": np.stack([m[0] for m in wq]),
        "wq_scales": np.stack([m[1] for m in wq]),
        "wk": (n((E, K, N)) / np.sqrt(K) / s[None, :, None]).astype(np.float32),
        "wv_words": np.stack([m[0] for m in wv]),
        "wv_scales": np.stack([m[1] for m in wv]),
        "bias": (0.3 * n((3 * N, E))).astype(np.float32),
        "offs": striped(slot_token),
    }


def reference(x_words, x_scales, wq_words, wq_scales, wk, wv_words, wv_scales, bias, offs):
    wq = np.stack([unpack_weight(wq_words[e], wq_scales[e], "e4m3") for e in range(E)])
    wkq = mxq(f64(wk), 1, "e4m3")
    wv = np.stack([unpack_weight(wv_words[e], wv_scales[e], "e4m3") for e in range(E)])
    idx = unstriped(offs)
    xq = unpack_weight(x_words, x_scales, "e4m3")[:, idx]
    y = np.concatenate([by_expert(w, xq) for w in (wq, wkq, wv)])
    y = y + np.repeat(f64(bias), C, axis=1)
    out = y
    return out

@@ -1,0 +1,152 @@
+from contextlib import ExitStack
+
+import concourse.mybir as mybir
+
+K, T, E, C, N = 1024, 512, 12, 128, 128
+FLOPS = 2 * K * 3 * N * E * C
+
+F32 = mybir.dt.float32
+BF16 = mybir.dt.bfloat16
+I32 = mybir.dt.int32
+U32 = mybir.dt.uint32
+U16 = mybir.dt.uint16
+U8 = mybir.dt.uint8
+FP8X4 = mybir.dt.float8_e4m3fn_x4
+ADD = mybir.AluOpType.add
+
+P = 128
+PACK = 4
+PASSES = K // (P * PACK)
+QUADS = 4
+ROWS = 4
+GATHER_EXPERTS = 3
+BANK_EXPERTS = 4
+LINE = 4
+
+
+def tile_moe_qkv_s_kernel(
+    tc, x_words, x_scales, wq_words, wq_scales, wk, wv_words, wv_scales, bias, offs, out
+):
+    nc = tc.nc
+    with ExitStack() as ctx:
+        keep = ctx.enter_context(tc.tile_pool(name="keep", bufs=1))
+        psum = ctx.enter_context(tc.psum_pool(name="psum", bufs=6))
+
+        x_win = keep.tile([P, PASSES, T], I32, name="x_win", align_bytes=64)
+        nc.sync.dma_start(out=x_win[:], in_=x_words.rearrange("s p t d -> p s (t d)").bitcast(I32))
+        offsets = keep.tile([P, E * C // 16], U16, name="offsets")
+        nc.sync.dma_start(offsets[:], offs)
+
+        xs_win = keep.tile([P, T], U8, name="xs_win", align_bytes=64)
+        nc.vector.memset(xs_win[:].bitcast(I32), 0)
+        for q in range(QUADS):
+            nc.scalar.dma_start(
+                out=xs_win[32 * q : 32 * q + PASSES * ROWS, :].bitcast(I32),
+                in_=x_scales[:, ROWS * q : ROWS * (q + 1), :].bitcast(I32),
+            )
+
+        q_planes = keep.tile([P, E * PASSES, N], U8, name="q_planes", align_bytes=64)
+        v_planes = keep.tile([P, E * PASSES, N], U8, name="v_planes", align_bytes=64)
+        V_ROW = 8
+        scale_loads = [(q_planes, wq_scales, 0, q) for q in range(QUADS)] + [
+            (v_planes, wv_scales, V_ROW, q) for q in range(QUADS)
+        ]
+        bias_sb = keep.tile([P, 3, E], F32, name="bias_sb")
+
+        wk_raw = []
+        for e in range(E):
+            raw = keep.tile([P, PASSES, PACK, N], F32, name=f"wk_raw{e}")
+            nc.sync.dma_start(out=raw[:], in_=wk[e].rearrange("(s p j) n -> p s j n", s=PASSES, j=PACK))
+            wk_raw.append(raw)
+            if e == 1:
+                nc.sync.dma_start(out=bias_sb[:], in_=bias.rearrange("(a p) e -> p a e", p=P))
+            if 2 <= e < 2 + len(scale_loads):
+                planes, scales, row0, q = scale_loads[e - 2]
+                nc.sync.dma_start(
+                    out=planes[32 * q + row0 : 32 * q + row0 + ROWS, :, :].bitcast(I32),
+                    in_=scales[:, :, ROWS * q : ROWS * (q + 1), :].rearrange("e s r n -> r (e s) n").bitcast(I32),
+                )
+
+        def load_words(words, label):
+            tiles = []
+            for g in range(E // BANK_EXPERTS):
+                w = keep.tile([P, BANK_EXPERTS * PASSES, N], I32, name=f"{label}{g}", align_bytes=64)
+                src = words[g * BANK_EXPERTS : (g + 1) * BANK_EXPERTS]
+                nc.sync.dma_start(out=w[:], in_=src.rearrange("e s p n d -> p (e s) (n d)").bitcast(I32))
+                tiles.append(w)
+            return tiles
+
+        q_words = load_words(wq_words, "q_words")
+        v_words = load_words(wv_words, "v_words")
+
+        slots = GATHER_EXPERTS * C
+        tok_words = []
+        tok_planes = []
+        for c in range(E // GATHER_EXPERTS):
+            cols = offsets[:, c * slots // 16 : (c + 1) * slots // 16]
+            per_pass = []
+            for s in range(PASSES):
+                g = keep.tile([P, slots], U32, name=f"tok_words{c}_{s}", align_bytes=64)
+                nc.vector.tensor_copy(g[:], x_win[:, s, :].bitcast(U32).indirect(cols))
+                per_pass.append(g)
+            gs = keep.tile([P, slots], U8, name=f"tok_planes{c}", align_bytes=64)
+            nc.vector.tensor_copy(gs[:], xs_win[:].indirect(cols))
+            tok_words.append(per_pass)
+            tok_planes.append(gs)
+
+        k_words = []
+        k_planes = []
+        for e in range(E):
+            grouped = keep.tile([P, PASSES, N, PACK], BF16, name=f"wk_bf{e}", align_bytes=64)
+            nc.scalar.copy(
+                out=grouped[:].rearrange("p s (c i) j -> p s c j i", i=LINE),
+                in_=wk_raw[e][:].rearrange("p s j (c i) -> p s c j i", i=LINE),
+            )
+            codes = keep.tile([P, PASSES * N], U32, name=f"k_words{e}", align_bytes=64)
+            plane = keep.tile([P, PASSES * N], U8, name=f"k_planes{e}", align_bytes=64)
+            nc.vector.quantize_mx(
+                out=codes[:].bitcast(FP8X4), scales=plane[:], in_=grouped[:].rearrange("p s n j -> p (s n j)")
+            )
+            k_words.append(codes)
+            k_planes.append(plane)
+
+        def weights(proj, e, s):
+            if proj == 1:
+                return k_words[e][:, s * N : (s + 1) * N], k_planes[e][:, s * N : (s + 1) * N]
+            g, u = divmod(e, BANK_EXPERTS)
+            if proj == 0:
+                return q_words[g][:, u * PASSES + s, :], q_planes[:, e * PASSES + s, :]
+            return v_words[g][:, u * PASSES + s, :], v_planes[V_ROW:P, e * PASSES + s, :]
+
+        for proj in (1, 0, 2):
+            res = keep.tile([P, E, C], F32, name=f"res{proj}")
+            for g in range(E // BANK_EXPERTS):
+                acc = psum.tile([P, BANK_EXPERTS, C], F32, name="acc")
+                for u in range(BANK_EXPERTS):
+                    e = g * BANK_EXPERTS + u
+                    c, o = divmod(e, GATHER_EXPERTS)
+                    for s in range(PASSES):
+                        w, ws = weights(proj, e, s)
+                        nc.tensor.matmul_mx(
+                            out=acc[:, u, :],
+                            lhsT=w.bitcast(FP8X4),
+                            lhsT_scale=ws,
+                            rhs=tok_words[c][s][:, o * C : (o + 1) * C].bitcast(FP8X4),
+                            rhs_scale=tok_planes[c][ROWS * s : P, o * C : (o + 1) * C],
+                            start=(s == 0),
+                            stop=(s == PASSES - 1),
+                        )
+                es = slice(g * BANK_EXPERTS, (g + 1) * BANK_EXPERTS)
+                nc.vector.tensor_tensor(
+                    out=res[:, es, :],
+                    in0=acc[:],
+                    in1=bias_sb[:, proj, es].unsqueeze(2).to_broadcast([P, BANK_EXPERTS, C]),
+                    op=ADD,
+                )
+                if proj == 2:
+                    nc.sync.dma_start(
+                        out=out[proj * N : (proj + 1) * N, g * BANK_EXPERTS * C : (g + 1) * BANK_EXPERTS * C],
+                        in_=res[:, es, :].rearrange("p e c -> p (e c)"),
+                    )
+            if proj != 2:
+                nc.sync.dma_start(out=out[proj * N : (proj + 1) * N, :], in_=res[:].rearrange("p e c -> p (e c)"))

@@ -22,6 +22,9 @@ ROWS = 4
 GATHER_EXPERTS = 3
 BANK_EXPERTS = 4
 LINE = 4
+GROUPS = ((4, 4, 4), (4, 4, 4), (4, 4, 2, 2))
+WK_LOADS = (2, 2, 2, 2, 2, 2)
+IDENT = mybir.ActivationFunctionType.Identity
 
 
 def tile_moe_qkv_s_kernel(
@@ -30,7 +33,7 @@ def tile_moe_qkv_s_kernel(
     nc = tc.nc
     with ExitStack() as ctx:
         keep = ctx.enter_context(tc.tile_pool(name="keep", bufs=1))
-        psum = ctx.enter_context(tc.psum_pool(name="psum", bufs=6))
+        psum = ctx.enter_context(tc.psum_pool(name="psum", bufs=8))
 
         x_win = keep.tile([P, PASSES, T], I32, name="x_win", align_bytes=64)
         nc.sync.dma_start(out=x_win[:], in_=x_words.rearrange("s p t d -> p s (t d)").bitcast(I32))
@@ -48,36 +51,40 @@ def tile_moe_qkv_s_kernel(
         q_planes = keep.tile([P, E * PASSES, N], U8, name="q_planes", align_bytes=64)
         v_planes = keep.tile([P, E * PASSES, N], U8, name="v_planes", align_bytes=64)
         V_ROW = 8
-        scale_loads = [(q_planes, wq_scales, 0, q) for q in range(QUADS)] + [
-            (v_planes, wv_scales, V_ROW, q) for q in range(QUADS)
+        scale_loads = [(q_planes, wq_scales, 0, r) for r in range(ROWS)] + [
+            (v_planes, wv_scales, V_ROW, r) for r in range(ROWS)
         ]
-        bias_sb = keep.tile([P, 3, E], F32, name="bias_sb")
+        bias_sb = keep.tile([P, 3, 16], F32, name="bias_sb")
 
         wk_raw = []
-        for e in range(E):
-            raw = keep.tile([P, PASSES, PACK, N], F32, name=f"wk_raw{e}")
-            nc.sync.dma_start(out=raw[:], in_=wk[e].rearrange("(s p j) n -> p s j n", s=PASSES, j=PACK))
-            wk_raw.append(raw)
-            if e == 1:
-                nc.sync.dma_start(out=bias_sb[:], in_=bias.rearrange("(a p) e -> p a e", p=P))
-            if 2 <= e < 2 + len(scale_loads):
-                planes, scales, row0, q = scale_loads[e - 2]
-                nc.sync.dma_start(
-                    out=planes[32 * q + row0 : 32 * q + row0 + ROWS, :, :].bitcast(I32),
-                    in_=scales[:, :, ROWS * q : ROWS * (q + 1), :].rearrange("e s r n -> r (e s) n").bitcast(I32),
-                )
+        e0 = 0
+        for i, width in enumerate(WK_LOADS):
+            raw = keep.tile([P, width * PASSES, PACK * N], F32, name=f"wk_raw{i}")
+            src = wk[e0 : e0 + width].rearrange("e (s p j) n -> p (e s) (j n)", s=PASSES, j=PACK)
+            nc.sync.dma_start(out=raw[:], in_=src)
+            for u in range(width):
+                wk_raw.append(raw[:, u * PASSES : (u + 1) * PASSES, :])
+            e0 = e0 + width
+            if i == 2:
+                nc.sync.dma_start(out=bias_sb[:, :, 0:E], in_=bias.rearrange("(a p) e -> p a e", p=P))
+            if i >= 2:
+                for planes, scales, row0, r in scale_loads[2 * (i - 2) : 2 * (i - 1)]:
+                    rows = scales.rearrange("e s (q r) n -> r q (e s) n", r=ROWS)
+                    nc.sync.dma_start(out=planes[row0 + r : P : 32, :, :].bitcast(I32), in_=rows[r].bitcast(I32))
 
-        def load_words(words, label):
+        def load_words(words, label, widths):
             tiles = []
-            for g in range(E // BANK_EXPERTS):
-                w = keep.tile([P, BANK_EXPERTS * PASSES, N], I32, name=f"{label}{g}", align_bytes=64)
-                src = words[g * BANK_EXPERTS : (g + 1) * BANK_EXPERTS]
+            first = 0
+            for g, width in enumerate(widths):
+                w = keep.tile([P, width * PASSES, N], I32, name=f"{label}{g}", align_bytes=64)
+                src = words[first : first + width]
                 nc.sync.dma_start(out=w[:], in_=src.rearrange("e s p n d -> p (e s) (n d)").bitcast(I32))
-                tiles.append(w)
+                tiles.extend(w[:, u * PASSES : (u + 1) * PASSES, :] for u in range(width))
+                first = first + width
             return tiles
 
-        q_words = load_words(wq_words, "q_words")
-        v_words = load_words(wv_words, "v_words")
+        q_words = load_words(wq_words, "q_words", GROUPS[0])
+        v_words = load_words(wv_words, "v_words", GROUPS[2])
 
         slots = GATHER_EXPERTS * C
         tok_words = []
@@ -100,7 +107,7 @@ def tile_moe_qkv_s_kernel(
             grouped = keep.tile([P, PASSES, N, PACK], BF16, name=f"wk_bf{e}", align_bytes=64)
             nc.scalar.copy(
                 out=grouped[:].rearrange("p s (c i) j -> p s c j i", i=LINE),
-                in_=wk_raw[e][:].rearrange("p s j (c i) -> p s c j i", i=LINE),
+                in_=wk_raw[e].rearrange("p s (j c i) -> p s c j i", j=PACK, i=LINE),
             )
             codes = keep.tile([P, PASSES * N], U32, name=f"k_words{e}", align_bytes=64)
             plane = keep.tile([P, PASSES * N], U8, name=f"k_planes{e}", align_bytes=64)
@@ -113,17 +120,17 @@ def tile_moe_qkv_s_kernel(
         def weights(proj, e, s):
             if proj == 1:
                 return k_words[e][:, s * N : (s + 1) * N], k_planes[e][:, s * N : (s + 1) * N]
-            g, u = divmod(e, BANK_EXPERTS)
             if proj == 0:
-                return q_words[g][:, u * PASSES + s, :], q_planes[:, e * PASSES + s, :]
-            return v_words[g][:, u * PASSES + s, :], v_planes[V_ROW:P, e * PASSES + s, :]
+                return q_words[e][:, s, :], q_planes[:, e * PASSES + s, :]
+            return v_words[e][:, s, :], v_planes[V_ROW:P, e * PASSES + s, :]
 
         for proj in (1, 0, 2):
             res = keep.tile([P, E, C], F32, name=f"res{proj}")
-            for g in range(E // BANK_EXPERTS):
+            first = 0
+            for width in GROUPS[proj]:
                 acc = psum.tile([P, BANK_EXPERTS, C], F32, name="acc")
-                for u in range(BANK_EXPERTS):
-                    e = g * BANK_EXPERTS + u
+                for u in range(width):
+                    e = first + u
                     c, o = divmod(e, GATHER_EXPERTS)
                     for s in range(PASSES):
                         w, ws = weights(proj, e, s)
@@ -136,17 +143,23 @@ def tile_moe_qkv_s_kernel(
                             start=(s == 0),
                             stop=(s == PASSES - 1),
                         )
-                es = slice(g * BANK_EXPERTS, (g + 1) * BANK_EXPERTS)
-                nc.vector.tensor_tensor(
-                    out=res[:, es, :],
-                    in0=acc[:],
-                    in1=bias_sb[:, proj, es].unsqueeze(2).to_broadcast([P, BANK_EXPERTS, C]),
-                    op=ADD,
-                )
+                es = slice(first, first + width)
+                if proj == 0:
+                    for u in range(width):
+                        e = first + u
+                        nc.scalar.activation(res[:, e, :], acc[:, u, :], IDENT, bias=bias_sb[:, proj, e : e + 1])
+                else:
+                    nc.vector.tensor_tensor(
+                        out=res[:, es, :],
+                        in0=acc[:, 0:width, :],
+                        in1=bias_sb[:, proj, es].unsqueeze(2).to_broadcast([P, width, C]),
+                        op=ADD,
+                    )
                 if proj == 2:
                     nc.sync.dma_start(
-                        out=out[proj * N : (proj + 1) * N, g * BANK_EXPERTS * C : (g + 1) * BANK_EXPERTS * C],
+                        out=out[proj * N : (proj + 1) * N, first * C : (first + width) * C],
                         in_=res[:, es, :].rearrange("p e c -> p (e c)"),
                     )
+                first = first + width
             if proj != 2:
                 nc.sync.dma_start(out=out[proj * N : (proj + 1) * N, :], in_=res[:].rearrange("p e c -> p (e c)"))

from contextlib import ExitStack

import concourse.mybir as mybir

K, T, E, C, N = 1024, 512, 12, 128, 128
FLOPS = 2 * K * 3 * N * E * C

F32 = mybir.dt.float32
BF16 = mybir.dt.bfloat16
I32 = mybir.dt.int32
U32 = mybir.dt.uint32
U16 = mybir.dt.uint16
U8 = mybir.dt.uint8
FP8X4 = mybir.dt.float8_e4m3fn_x4
ADD = mybir.AluOpType.add

P = 128
PACK = 4
PASSES = K // (P * PACK)
QUADS = 4
ROWS = 4
GATHER_EXPERTS = 3
BANK_EXPERTS = 4
LINE = 4
GROUPS = ((4, 4, 4), (4, 4, 4), (4, 4, 2, 2))
WK_LOADS = (2, 2, 2, 2, 2, 2)
IDENT = mybir.ActivationFunctionType.Identity


def tile_moe_qkv_s_kernel(
    tc, x_words, x_scales, wq_words, wq_scales, wk, wv_words, wv_scales, bias, offs, out
):
    nc = tc.nc
    with ExitStack() as ctx:
        keep = ctx.enter_context(tc.tile_pool(name="keep", bufs=1))
        psum = ctx.enter_context(tc.psum_pool(name="psum", bufs=8))

        x_win = keep.tile([P, PASSES, T], I32, name="x_win", align_bytes=64)
        nc.sync.dma_start(out=x_win[:], in_=x_words.rearrange("s p t d -> p s (t d)").bitcast(I32))
        offsets = keep.tile([P, E * C // 16], U16, name="offsets")
        nc.sync.dma_start(offsets[:], offs)

        xs_win = keep.tile([P, T], U8, name="xs_win", align_bytes=64)
        nc.vector.memset(xs_win[:].bitcast(I32), 0)
        for q in range(QUADS):
            nc.scalar.dma_start(
                out=xs_win[32 * q : 32 * q + PASSES * ROWS, :].bitcast(I32),
                in_=x_scales[:, ROWS * q : ROWS * (q + 1), :].bitcast(I32),
            )

        q_planes = keep.tile([P, E * PASSES, N], U8, name="q_planes", align_bytes=64)
        v_planes = keep.tile([P, E * PASSES, N], U8, name="v_planes", align_bytes=64)
        V_ROW = 8
        scale_loads = [(q_planes, wq_scales, 0, r) for r in range(ROWS)] + [
            (v_planes, wv_scales, V_ROW, r) for r in range(ROWS)
        ]
        bias_sb = keep.tile([P, 3, 16], F32, name="bias_sb")

        wk_raw = []
        e0 = 0
        for i, width in enumerate(WK_LOADS):
            raw = keep.tile([P, width * PASSES, PACK * N], F32, name=f"wk_raw{i}")
            src = wk[e0 : e0 + width].rearrange("e (s p j) n -> p (e s) (j n)", s=PASSES, j=PACK)
            nc.sync.dma_start(out=raw[:], in_=src)
            for u in range(width):
                wk_raw.append(raw[:, u * PASSES : (u + 1) * PASSES, :])
            e0 = e0 + width
            if i == 2:
                nc.sync.dma_start(out=bias_sb[:, :, 0:E], in_=bias.rearrange("(a p) e -> p a e", p=P))
            if i >= 2:
                for planes, scales, row0, r in scale_loads[2 * (i - 2) : 2 * (i - 1)]:
                    rows = scales.rearrange("e s (q r) n -> r q (e s) n", r=ROWS)
                    nc.sync.dma_start(out=planes[row0 + r : P : 32, :, :].bitcast(I32), in_=rows[r].bitcast(I32))

        def load_words(words, label, widths):
            tiles = []
            first = 0
            for g, width in enumerate(widths):
                w = keep.tile([P, width * PASSES, N], I32, name=f"{label}{g}", align_bytes=64)
                src = words[first : first + width]
                nc.sync.dma_start(out=w[:], in_=src.rearrange("e s p n d -> p (e s) (n d)").bitcast(I32))
                tiles.extend(w[:, u * PASSES : (u + 1) * PASSES, :] for u in range(width))
                first = first + width
            return tiles

        q_words = load_words(wq_words, "q_words", GROUPS[0])
        v_words = load_words(wv_words, "v_words", GROUPS[2])

        slots = GATHER_EXPERTS * C
        tok_words = []
        tok_planes = []
        for c in range(E // GATHER_EXPERTS):
            cols = offsets[:, c * slots // 16 : (c + 1) * slots // 16]
            per_pass = []
            for s in range(PASSES):
                g = keep.tile([P, slots], U32, name=f"tok_words{c}_{s}", align_bytes=64)
                nc.vector.tensor_copy(g[:], x_win[:, s, :].bitcast(U32).indirect(cols))
                per_pass.append(g)
            gs = keep.tile([P, slots], U8, name=f"tok_planes{c}", align_bytes=64)
            nc.vector.tensor_copy(gs[:], xs_win[:].indirect(cols))
            tok_words.append(per_pass)
            tok_planes.append(gs)

        k_words = []
        k_planes = []
        for e in range(E):
            grouped = keep.tile([P, PASSES, N, PACK], BF16, name=f"wk_bf{e}", align_bytes=64)
            nc.scalar.copy(
                out=grouped[:].rearrange("p s (c i) j -> p s c j i", i=LINE),
                in_=wk_raw[e].rearrange("p s (j c i) -> p s c j i", j=PACK, i=LINE),
            )
            codes = keep.tile([P, PASSES * N], U32, name=f"k_words{e}", align_bytes=64)
            plane = keep.tile([P, PASSES * N], U8, name=f"k_planes{e}", align_bytes=64)
            nc.vector.quantize_mx(
                out=codes[:].bitcast(FP8X4), scales=plane[:], in_=grouped[:].rearrange("p s n j -> p (s n j)")
            )
            k_words.append(codes)
            k_planes.append(plane)

        def weights(proj, e, s):
            if proj == 1:
                return k_words[e][:, s * N : (s + 1) * N], k_planes[e][:, s * N : (s + 1) * N]
            if proj == 0:
                return q_words[e][:, s, :], q_planes[:, e * PASSES + s, :]
            return v_words[e][:, s, :], v_planes[V_ROW:P, e * PASSES + s, :]

        for proj in (1, 0, 2):
            res = keep.tile([P, E, C], F32, name=f"res{proj}")
            first = 0
            for width in GROUPS[proj]:
                acc = psum.tile([P, BANK_EXPERTS, C], F32, name="acc")
                for u in range(width):
                    e = first + u
                    c, o = divmod(e, GATHER_EXPERTS)
                    for s in range(PASSES):
                        w, ws = weights(proj, e, s)
                        nc.tensor.matmul_mx(
                            out=acc[:, u, :],
                            lhsT=w.bitcast(FP8X4),
                            lhsT_scale=ws,
                            rhs=tok_words[c][s][:, o * C : (o + 1) * C].bitcast(FP8X4),
                            rhs_scale=tok_planes[c][ROWS * s : P, o * C : (o + 1) * C],
                            start=(s == 0),
                            stop=(s == PASSES - 1),
                        )
                es = slice(first, first + width)
                if proj == 0:
                    for u in range(width):
                        e = first + u
                        nc.scalar.activation(res[:, e, :], acc[:, u, :], IDENT, bias=bias_sb[:, proj, e : e + 1])
                else:
                    nc.vector.tensor_tensor(
                        out=res[:, es, :],
                        in0=acc[:, 0:width, :],
                        in1=bias_sb[:, proj, es].unsqueeze(2).to_broadcast([P, width, C]),
                        op=ADD,
                    )
                if proj == 2:
                    nc.sync.dma_start(
                        out=out[proj * N : (proj + 1) * N, first * C : (first + width) * C],
                        in_=res[:, es, :].rearrange("p e c -> p (e c)"),
                    )
                first = first + width
            if proj != 2:
                nc.sync.dma_start(out=out[proj * N : (proj + 1) * N, :], in_=res[:].rearrange("p e c -> p (e c)"))
